import numpy as np
import ml_dtypes


def mxq(x, axis, fmt="e4m3"):
    dtype, down = {"e4m3": (ml_dtypes.float8_e4m3fn, 7), "e5m2": (ml_dtypes.float8_e5m2, 14)}[fmt]
    v = np.moveaxis(np.asarray(x, np.float32).astype(ml_dtypes.bfloat16).astype(np.float64), axis, -1)
    blocks = v.reshape(v.shape[:-1] + (-1, 32))
    amax = np.abs(blocks).max(-1, keepdims=True)
    byte = np.maximum(np.where(amax > 0, np.frexp(amax)[1] - 1 + 127, 0) - down, 1)
    scale = np.exp2(byte - 127.0)
    codes = (blocks / scale).astype(np.float32).astype(dtype).astype(np.float64)
    return np.moveaxis((codes * scale).reshape(v.shape), -1, axis)


WIDE = False


def mx_kscale(k):
    if not WIDE:
        return np.ones(k)
    levels = np.array([10, -10, 5, -5, 0])
    if k % 512:
        return np.exp2(np.random.permutation(np.resize(levels, k // 32))).repeat(32)
    a = np.empty((k // 512, 16))
    for p in range(k // 512):
        a[p, :8] = np.random.permutation(np.resize(levels, 8))
        for g in range(8):
            far = levels[np.abs(levels - a[p, g]) >= 10]
            a[p, g + 8] = far[np.random.randint(len(far))]
    return np.exp2(a.ravel()).repeat(32)


def f64(x):
    return np.asarray(x).astype(np.float64)


E2M1 = np.array([0.0, 0.5, 1.0, 1.5, 2.0, 3.0, 4.0, 6.0, -0.0, -0.5, -1.0, -1.5, -2.0, -3.0, -4.0, -6.0])


def pack_weight(w, fmt):
    k, n = w.shape
    w = f64(np.asarray(w, np.float32).astype(ml_dtypes.bfloat16)).reshape(k // 32, 32, n)
    amax = np.abs(w).max(1)
    if fmt == "e4m3":
        byte = np.frexp(amax)[1] - 1 + 127 - 7
    else:
        mant, ex = np.frexp(amax / 6.0)
        byte = np.where(mant > 0.5, ex, ex - 1) + 127
    byte = np.clip(np.where(amax > 0, byte, 1), 1, 254)
    scaled = (w * np.exp2(127.0 - byte)[:, None, :]).reshape(k, n).astype(np.float32)
    by_word = np.ascontiguousarray(scaled.reshape(k // 512, 128, 4, n).transpose(0, 1, 3, 2))
    if fmt == "e4m3":
        words = by_word.astype(ml_dtypes.float8_e4m3fn).view(np.uint8)
    else:
        c = by_word.astype(ml_dtypes.float4_e2m1fn).view(np.uint8) & 0xF
        words = (c[..., 0::2] | (c[..., 1::2] << 4)).reshape(k // 512, 128, 2 * n)
    return np.ascontiguousarray(words), np.ascontiguousarray(byte.astype(np.uint8).reshape(k // 512, 16, n))


def unpack_weight(words, scales, fmt):
    g, _, n = scales.shape
    words = np.ascontiguousarray(words).reshape(g, 128, n, -1)
    if fmt == "e4m3":
        vals = words.view(ml_dtypes.float8_e4m3fn).astype(np.float64)
    else:
        nib = np.empty((g, 128, n, 4), np.uint8)
        nib[..., 0::2] = words & 0xF
        nib[..., 1::2] = words >> 4
        vals = E2M1[nib]
    vals = vals * np.repeat(np.exp2(scales.astype(np.float64) - 127.0), 8, axis=1)[..., None]
    return vals.transpose(0, 1, 3, 2).reshape(g * 512, n)


K, M, T = 1024, 512, 512


def setup_inputs():
    n = np.random.standard_normal
    s = mx_kscale(K)[:, None]
    u = mx_kscale(T)[:, None]
    q = n((K, T)) * s
    p_vc = pack_weight(0.1 * n((T, M)) / u, "e2m1")
    return {
        "qc": (q).astype(np.float32),
        "kc": (n((K, T)) / np.sqrt(K) / s).astype(np.float32),
        "qd": (q * 0.995 ** (np.arange(T) + 1.0)).astype(np.float32),
        "st": (n((K, M)) / np.sqrt(K) / s).astype(np.float32),
        "vc_words": p_vc[0],
        "vc_scales": p_vc[1],
        "dm": (np.tril(0.995 ** (np.arange(T)[:, None] - np.arange(T)[None])).T * u).astype(np.float32),
        "g": (n((512, 512))).astype(np.float32),
    }


def reference(qc, kc, qd, st, vc_words, vc_scales, dm, g):
    qc_ = mxq(f64(qc), 0, "e4m3")
    kc_ = mxq(f64(kc), 0, "e4m3")
    qd_ = mxq(f64(qd), 0, "e4m3")
    st_ = mxq(f64(st), 0, "e4m3")
    vc_ = unpack_weight(vc_words, vc_scales, "e2m1")
    h_ = mxq((kc_.T @ qc_) * f64(dm), 0, "e4m3")
    y = vc_.T @ h_ + st_.T @ qd_
    return f64(g) * y

from contextlib import ExitStack

import concourse.mybir as mybir

K, M, T = 1024, 512, 512
FLOPS = 2 * K * T * T + 2 * T * M * T + 2 * K * M * T

F32 = mybir.dt.float32
BF16 = mybir.dt.bfloat16
I32 = mybir.dt.int32
U32 = mybir.dt.uint32
U8 = mybir.dt.uint8
FP8X4 = mybir.dt.float8_e4m3fn_x4
FP4X4 = mybir.dt.float4_e2m1fn_x4
MULT = mybir.AluOpType.mult

P = 128
PACK = 4
K_PASS = P * PACK
HALF = 256


def tile_mix_linattn_fm_mul_kernel(tc, qc, kc, qd, st, vc_words, vc_scales, dm, g, out):
    nc = tc.nc

    with ExitStack() as ctx:
        sb = ctx.enter_context(tc.tile_pool(name="sb", bufs=1))
        psum = ctx.enter_context(tc.psum_pool(name="psum", bufs=1))
        ctx.enter_context(tc.manual_schedule())

        def load_rows(name, rows):
            raw = sb.tile([P, PACK, rows.shape[1]], F32, name=name)
            nc.sync.dma_start(out=raw[:], in_=rows.rearrange("(p j) w -> p j w", j=PACK))
            return raw

        def mx_tiles(name):
            codes = sb.tile([P, 512], U32, name=name + "_codes", align_bytes=64)
            scales = sb.tile([P, 512], U8, name=name + "_scales", align_bytes=64)
            return codes, scales

        def copy(on_scalar, dst, src):
            if on_scalar:
                nc.scalar.copy(out=dst, in_=src)
            else:
                nc.vector.tensor_copy(out=dst, in_=src)

        def interleave(name, on_scalar, src, dtype):
            width = src.shape[2]
            grouped = sb.tile([P, width, PACK], dtype, name=name, align_bytes=64)
            copy(on_scalar, grouped[:].rearrange("p (c i) j -> p c j i", i=4), src.rearrange("p j (c i) -> p c j i", i=4))
            return grouped

        def interleave_keys(name, on_scalar, raw, i0):
            grouped = sb.tile([P, 2, P, PACK], BF16, name=name, align_bytes=64)
            src = raw[:].rearrange("p j (m i) -> p m j i", i=PACK)[:, :, :, i0 : i0 + 2]
            copy(on_scalar, grouped[:].rearrange("p i m j -> p m j i"), src)
            return grouped

        def quantize(mx, col0, flat):
            codes, scales = mx
            cols = slice(col0, col0 + flat.shape[1] // PACK)
            nc.vector.quantize_mx(out=codes[:, cols].bitcast(FP8X4), scales=scales[:, cols], in_=flat)

        def flat3(grouped):
            return grouped[:].rearrange("p w j -> p (w j)")

        vc_plane = sb.tile([P, M], U8, name="vc_plane", align_bytes=64)
        vc_codes = sb.tile([P, 2 * M], U8, name="vc_codes", align_bytes=64)
        nc.vector.memset(vc_plane[:].bitcast(I32), 0)
        kc_raw = [None, None]
        qc_raw = [None, None]
        kc_raw[0] = load_rows("kc_raw0", kc[0:K_PASS, :])
        qc_raw[0] = load_rows("qc_raw0", qc[0:K_PASS, :])
        kc_raw[1] = load_rows("kc_raw1", kc[K_PASS:K, :])
        nc.scalar.dma_start(out=vc_codes[:].bitcast(I32), in_=vc_words[0].bitcast(I32))
        for q in range(4):
            nc.scalar.dma_start(
                out=vc_plane[32 * q : 32 * q + 4, :].bitcast(I32),
                in_=vc_scales[0, 4 * q : 4 * q + 4, :].bitcast(I32),
            )
        qc_raw[1] = load_rows("qc_raw1", qc[K_PASS:K, :])
        dm_raw = load_rows("dm_raw", dm)
        qd_raw0 = load_rows("qd_raw0", qd[0:K_PASS, :])
        st_raw0 = load_rows("st_raw0", st[0:K_PASS, :])
        qd_raw1 = load_rows("qd_raw1", qd[K_PASS:K, :])
        st_raw1 = [load_rows("st_raw1_%d" % h, st[K_PASS:K, h * HALF : (h + 1) * HALF]) for h in range(2)]
        g_sb = []
        for n in range(4):
            g_tile = sb.tile([P, T], F32, name="g%d" % n)
            nc.sync.dma_start(out=g_tile[:], in_=g[n * P : (n + 1) * P, :])
            g_sb.append(g_tile)

        def quantize_plain(name, raw):
            mx = mx_tiles(name)
            lo = interleave(name + "_lo", True, raw[:, :, 0:HALF], BF16)
            hi = interleave(name + "_hi", False, raw[:, :, HALF:], BF16)
            quantize(mx, HALF, flat3(hi))
            quantize(mx, 0, flat3(lo))
            return mx

        def mm(acc, lhs_codes, lhs_scales, rhs_codes, rhs_scales, start, stop):
            nc.tensor.matmul_mx(
                out=acc, lhsT=lhs_codes, lhsT_scale=lhs_scales, rhs=rhs_codes, rhs_scale=rhs_scales, start=start, stop=stop
            )

        kc_mx = []
        qc_mx = []
        for a in range(2):
            mx = mx_tiles("kc%d" % a)
            lo = interleave_keys("kc_lo%d" % a, True, kc_raw[a], 0)
            hi = interleave_keys("kc_hi%d" % a, False, kc_raw[a], 2)
            quantize(mx, HALF, hi[:].rearrange("p i m j -> p (i m j)"))
            quantize(mx, 0, lo[:].rearrange("p i m j -> p (i m j)"))
            kc_mx.append(mx)
            qc_mx.append(quantize_plain("qc%d" % a, qc_raw[a]))

        h_mx = mx_tiles("h")
        h_bf = {}
        order = [2, 3, 0, 1]
        for b in order:
            t_cols = slice(b * P, (b + 1) * P)
            dm_words = interleave("dm%d" % b, True, dm_raw[:, :, t_cols], F32)
            scores = psum.tile([P, PACK, P], F32, name="scores%d" % b)
            for i in range(PACK):
                for a in range(2):
                    i_cols = slice(i * P, (i + 1) * P)
                    mm(
                        scores[:, i, :],
                        kc_mx[a][0][:, i_cols].bitcast(FP8X4), kc_mx[a][1][:, i_cols],
                        qc_mx[a][0][:, t_cols].bitcast(FP8X4), qc_mx[a][1][:, t_cols],
                        a == 0, a == 1,
                    )
            if b % 2 == 0:
                pair = sb.tile([P, HALF, PACK], BF16, name="h_bf%d" % b, align_bytes=64)
                h_bf[b // 2] = pair
            nc.vector.tensor_tensor(
                out=h_bf[b // 2][:, (b % 2) * P : (b % 2 + 1) * P, :],
                in0=scores[:].rearrange("p i t -> p t i"),
                in1=dm_words[:],
                op=MULT,
            )
            if b == 0:
                quantize(h_mx, HALF, flat3(h_bf[1]))

        qd0_lo = interleave("qd0_lo", True, qd_raw0[:, :, 0:HALF], BF16)
        qd0_hi = interleave("qd0_hi", False, qd_raw0[:, :, HALF:], BF16)
        quantize(h_mx, 0, flat3(h_bf[0]))
        qd0 = mx_tiles("qd0")
        quantize(qd0, HALF, flat3(qd0_hi))
        quantize(qd0, 0, flat3(qd0_lo))

        acc = []
        for n in range(4):
            y_tile = psum.tile([P, T], F32, name="y%d" % n)
            acc.append(y_tile)
            mm(
                y_tile[:],
                vc_codes[:, 2 * P * n : 2 * P * (n + 1)].bitcast(FP4X4), vc_plane[:, n * P : (n + 1) * P],
                h_mx[0][:].bitcast(FP8X4), h_mx[1][:], True, False,
            )

        def state_pass(n, st_mx, qd_mx, stop):
            n_cols = slice(n * P, (n + 1) * P)
            mm(
                acc[n][:],
                st_mx[0][:, n_cols].bitcast(FP8X4), st_mx[1][:, n_cols],
                qd_mx[0][:].bitcast(FP8X4), qd_mx[1][:], False, stop,
            )

        st0 = quantize_plain("st0", st_raw0)
        for n in order:
            state_pass(n, st0, qd0, False)
        qd1 = quantize_plain("qd1", qd_raw1)

        st1 = mx_tiles("st1")
        for h in range(2):
            lo = interleave("st1_lo%d" % h, True, st_raw1[h][:, :, 0:P], BF16)
            hi = interleave("st1_hi%d" % h, False, st_raw1[h][:, :, P:], BF16)
            quantize(st1, h * HALF + P, flat3(hi))
            quantize(st1, h * HALF, flat3(lo))
            state_pass(2 * h, st1, qd1, True)
            state_pass(2 * h + 1, st1, qd1, True)

        for n in range(4):
            result = sb.tile([P, T], F32, name="result%d" % n)
            nc.vector.tensor_tensor(out=result[:], in0=acc[n][:], in1=g_sb[n][:], op=MULT)
            nc.sync.dma_start(out=out[n * P : (n + 1) * P, :], in_=result[:])
